import numpy as np, ml_dtypes
CORES = [68,69,70,71,76,77,78,79,84,85,86,87]
N = 12
KT, F = 2, 512
def setup_inputs(rng):
    return {"a": rng.standard_normal((N, 128, KT * 128), dtype=np.float32).astype(ml_dtypes.bfloat16), "w": rng.standard_normal((N, 128, KT * F), dtype=np.float32).astype(ml_dtypes.bfloat16)}
def reference(a, w):
    tot = np.zeros((128, F))
    for j in range(N):
        for t in range(KT):
            tot += a[j][:, 128 * t:128 * t + 128].astype(np.float64).T @ w[j][:, F * t:F * t + F].astype(np.float64)
    s = tot.astype(ml_dtypes.bfloat16 if a.dtype != np.float64 else np.float64)
    return {"y": np.broadcast_to(s, (N,) + s.shape)}

@@ -1,0 +1,173 @@
+from concourse.bass import DstId, RemoteDMATransfer
+
+KT, F = 2, 512
+NP = 4
+PW = F // NP
+MAXR = 4
+MAXC = 3
+ADD = 1
+
+SCRATCH = {
+    "a_sb": ("sbuf", [128, KT * 128], "bfloat16"),
+    "w_sb": ("sbuf", [128, KT * F], "bfloat16"),
+    "p_sb": ("sbuf", [128, F], "bfloat16"),
+    "land1": ("dram", [MAXR, 128, PW], "bfloat16"),
+    "land2": ("dram", [MAXC, 128, PW], "bfloat16"),
+    "fin": ("dram", [NP, 128, PW], "bfloat16"),
+}
+for _q in range(NP):
+    SCRATCH["ps%d" % _q] = ("psum", [128, 512], "float32")
+
+SEMAPHORES = (["ld_a", "ld_w0", "ld_w1", "cp", "s1", "s2", "loc", "st_a", "st_b"]
+              + ["mm%d" % _q for _q in range(NP)] + ["s3_%d" % _q for _q in range(NP)])
+
+
+def _bits(mask):
+    return [1 << i for i in range(mask.bit_length()) if (mask >> i) & 1]
+
+
+def _parts(mask, n):
+    b = _bits(mask)
+    k = len(b) // n
+    return [sum(b[i * k:(i + 1) * k]) for i in range(n)]
+
+
+def _count(mask):
+    return len(_bits(mask))
+
+
+def _plan(T, topo):
+    ranks = list(T.cores)
+    chips = sorted(set(topo.chip(c) for c in ranks))
+    every = range(topo.CHIPS * topo.CORES_PER_CHIP)
+    on = dict((ch, [c for c in every if topo.chip(c) == ch]) for ch in chips)
+    plan = {}
+    for ch in chips:
+        away = [d for o in chips if o != ch for d in on[o]]
+        ports = [c for c in on[ch] if all(topo.may_write(c, d) for d in away)]
+        ports.sort(key=lambda c: (topo.die(c), c))
+        dies = sorted(set(topo.die(c) for c in ports))
+        per_die = NP // len(dies)
+        snd = [c for d in dies for c in [p for p in ports if topo.die(p) == d][:per_die]]
+        rk = [c for c in ranks if topo.chip(c) == ch]
+        helpers = [c for c in on[ch] if c not in rk]
+        idle = [h for h in helpers if h not in snd]
+        fld = [None] * NP
+        hq = [q for q in range(NP) if snd[q] in helpers]
+        for q in range(NP):
+            if q not in hq:
+                fld[q] = idle.pop(0)
+        for i, q in enumerate(hq):
+            fld[q] = snd[hq[(i + 1) % len(hq)]] if len(hq) > 1 else idle.pop(0)
+        plan[ch] = {"ranks": rk, "snd": snd, "fld": fld}
+    return chips, plan
+
+
+def _dst(topo, c):
+    rid, pid, _se = topo.addr(c)
+    return DstId(rid=rid, pnc=pid)
+
+
+def rank_program(g, core, T, topo):
+    chips, plan = _plan(T, topo)
+    ch = topo.chip(core)
+    if ch not in plan:
+        return
+    me = plan[ch]
+    is_rank = core in me["ranks"]
+    my_send = [q for q in range(NP) if me["snd"][q] == core]
+    my_fold = [q for q in range(NP) if me["fld"][q] == core]
+    if not (is_rank or my_send or my_fold):
+        return
+    S = T.sem
+    loc = 0
+
+    def cols(q):
+        return slice(q * PW, (q + 1) * PW)
+
+    if is_rank:
+        slot = me["ranks"].index(core)
+        g.sync.dma_start(T.a_sb[:], T.a[:]).then_inc(S.ld_a, 16)
+        g.scalar.dma_start(T.w_sb[:, 0:F], T.w[:, 0:F]).then_inc(S.ld_w0, 16)
+        g.sync.dma_start(T.w_sb[:, F:2 * F], T.w[:, F:2 * F]).then_inc(S.ld_w1, 16)
+        te = g.tensor
+        te.wait_ge(S.ld_a, 16)
+        te.wait_ge(S.ld_w0, 16)
+        for q in range(NP):
+            te.matmul(T["ps%d" % q][:, 0:PW], T.a_sb[:, 0:128], T.w_sb[:, cols(q)], start=True, stop=False)
+        te.wait_ge(S.ld_w1, 16)
+        for q in range(NP):
+            te.matmul(T["ps%d" % q][:, 0:PW], T.a_sb[:, 128:256], T.w_sb[:, F + q * PW:F + (q + 1) * PW],
+                      start=False, stop=True).then_inc(S["mm%d" % q], 1)
+        for q in range(NP):
+            g.vector.wait_ge(S["mm%d" % q], 1)
+            g.vector.tensor_copy(T.p_sb[:, cols(q)], T["ps%d" % q][:, 0:PW]).then_inc(S.cp, 1)
+
+        for q in my_send:
+            g.sync.wait_ge(S.cp, NP)
+            g.sync.dma_start(T.land1[slot], T.p_sb[:, cols(q)]).then_inc(S.s1, 16)
+        g.wait_ge(S.cp, NP)
+        trs = []
+        for q in range(NP):
+            d = me["snd"][q]
+            if d == core:
+                continue
+            m = _parts(topo.mask(core, d), NP)[len(trs)]
+            trs.append(RemoteDMATransfer(dst_ids=[_dst(topo, d)], dma_engine_mask=m, remote_sem=S.s1,
+                                         src=T.p_sb[:, cols(q)], dst=T.land1[slot]))
+            loc += _count(m)
+        g.remote_dma_fused(trs, local_sem=S.loc)
+
+    for q in my_send:
+        need = 0
+        for r in me["ranks"]:
+            need += 16 if r == core else _count(_parts(topo.mask(r, core), NP)[0])
+        g.wait_ge(S.s1, need)
+        srcs = [T.land1[i] for i in range(len(me["ranks"]))]
+        far = [plan[o]["fld"][q] for o in chips if o != ch]
+        near = me["fld"][q]
+        m_far = topo.mask(core, near)
+        for d in far:
+            m_far &= topo.mask(core, d)
+        m_near = topo.mask(core, near) & ~m_far
+        k = chips.index(ch)
+        trs = [RemoteDMATransfer(dst_ids=[_dst(topo, d) for d in far], dma_engine_mask=m_far, remote_sem=S.s2,
+                                 srcs=srcs, dsts=[T.land2[k] for d in far], alu_op=ADD),
+               RemoteDMATransfer(dst_ids=[_dst(topo, near)], dma_engine_mask=m_near, remote_sem=S.s2,
+                                 srcs=srcs, dsts=[T.land2[k]], alu_op=ADD)]
+        g.remote_dma_fused(trs, local_sem=S.loc)
+        loc += _count(m_far) + _count(m_near)
+
+    for q in my_fold:
+        need = 0
+        for o in chips:
+            s = plan[o]["snd"][q]
+            m_far = topo.mask(s, plan[o]["fld"][q])
+            for o2 in chips:
+                if o2 != o:
+                    m_far &= topo.mask(s, plan[o2]["fld"][q])
+            need += _count(m_far) if o != ch else _count(topo.mask(s, core) & ~m_far)
+        g.wait_ge(S.s2, need)
+        m = topo.mask(core, me["ranks"][0])
+        for r in me["ranks"]:
+            m &= topo.mask(core, r)
+        g.remote_dma_fused([RemoteDMATransfer(dst_ids=[_dst(topo, r) for r in me["ranks"]], dma_engine_mask=m,
+                                              remote_sem=S["s3_%d" % q], srcs=[T.land2[i] for i in range(len(chips))],
+                                              dsts=[T.fin[q] for r in me["ranks"]], alu_op=ADD)], local_sem=S.loc)
+        loc += _count(m)
+
+    if is_rank:
+        n = [0, 0]
+        for q in range(NP):
+            f = me["fld"][q]
+            m = topo.mask(f, core)
+            for r in me["ranks"]:
+                m &= topo.mask(f, r)
+            qu, st = ((g.sync, S.st_a), (g.scalar, S.st_b))[q % 2]
+            qu.wait_ge(S["s3_%d" % q], _count(m))
+            qu.dma_start(T.y[:, cols(q)], T.fin[q]).then_inc(st, 16)
+            n[q % 2] += 16
+        g.sync.wait_ge(S.st_a, n[0])
+        g.scalar.wait_ge(S.st_b, n[1])
+
+    g.wait_ge(S.loc, loc)

@@ -3,6 +3,9 @@ from concourse.bass import DstId, RemoteDMATransfer
 KT, F = 2, 512
 NP = 4
 PW = F // NP
+NW = 2
+PPW = NP // NW
+WW = F // NW
 MAXR = 4
 MAXC = 3
 ADD = 1
@@ -18,7 +21,9 @@ SCRATCH = {
 for _q in range(NP):
     SCRATCH["ps%d" % _q] = ("psum", [128, 512], "float32")
 
-SEMAPHORES = (["ld_a", "ld_w0", "ld_w1", "cp", "s1", "s2", "loc", "st_a", "st_b"]
+SEMAPHORES = (["ld_a", "s1", "s2", "loc", "st_a", "st_b"]
+              + ["ld_w%d%d" % (_t, _v) for _t in range(KT) for _v in range(NW)]
+              + ["cp%d" % _v for _v in range(NW)]
               + ["mm%d" % _q for _q in range(NP)] + ["s3_%d" % _q for _q in range(NP)])
 
 
@@ -45,10 +50,9 @@ def _plan(T, topo):
     for ch in chips:
         away = [d for o in chips if o != ch for d in on[o]]
         ports = [c for c in on[ch] if all(topo.may_write(c, d) for d in away)]
-        ports.sort(key=lambda c: (topo.die(c), c))
         dies = sorted(set(topo.die(c) for c in ports))
-        per_die = NP // len(dies)
-        snd = [c for d in dies for c in [p for p in ports if topo.die(p) == d][:per_die]]
+        by_die = [sorted(p for p in ports if topo.die(p) == d) for d in dies]
+        snd = [by_die[d][i] for i in range(NP // len(dies)) for d in range(len(dies))]
         rk = [c for c in ranks if topo.chip(c) == ch]
         helpers = [c for c in on[ch] if c not in rk]
         idle = [h for h in helpers if h not in snd]
@@ -88,40 +92,45 @@ def rank_program(g, core, T, topo):
     if is_rank:
         slot = me["ranks"].index(core)
         g.sync.dma_start(T.a_sb[:], T.a[:]).then_inc(S.ld_a, 16)
-        g.scalar.dma_start(T.w_sb[:, 0:F], T.w[:, 0:F]).then_inc(S.ld_w0, 16)
-        g.sync.dma_start(T.w_sb[:, F:2 * F], T.w[:, F:2 * F]).then_inc(S.ld_w1, 16)
+        for v in range(NW):
+            for t in range(KT):
+                qu = (g.scalar, g.sync)[t % 2]
+                c0 = t * F + v * WW
+                qu.dma_start(T.w_sb[:, c0:c0 + WW], T.w[:, c0:c0 + WW]).then_inc(S["ld_w%d%d" % (t, v)], 16)
         te = g.tensor
         te.wait_ge(S.ld_a, 16)
-        te.wait_ge(S.ld_w0, 16)
-        for q in range(NP):
-            te.matmul(T["ps%d" % q][:, 0:PW], T.a_sb[:, 0:128], T.w_sb[:, cols(q)], start=True, stop=False)
-        te.wait_ge(S.ld_w1, 16)
-        for q in range(NP):
-            te.matmul(T["ps%d" % q][:, 0:PW], T.a_sb[:, 128:256], T.w_sb[:, F + q * PW:F + (q + 1) * PW],
-                      start=False, stop=True).then_inc(S["mm%d" % q], 1)
+        for v in range(NW):
+            for t in range(KT):
+                te.wait_ge(S["ld_w%d%d" % (t, v)], 16)
+                for q in range(v * PPW, (v + 1) * PPW):
+                    mm = te.matmul(T["ps%d" % q][:, 0:PW], T.a_sb[:, t * 128:(t + 1) * 128],
+                                   T.w_sb[:, t * F + q * PW:t * F + (q + 1) * PW], start=(t == 0), stop=(t == KT - 1))
+                    if t == KT - 1:
+                        mm.then_inc(S["mm%d" % q], 1)
         for q in range(NP):
             g.vector.wait_ge(S["mm%d" % q], 1)
-            g.vector.tensor_copy(T.p_sb[:, cols(q)], T["ps%d" % q][:, 0:PW]).then_inc(S.cp, 1)
+            g.vector.tensor_copy(T.p_sb[:, cols(q)], T["ps%d" % q][:, 0:PW]).then_inc(S["cp%d" % (q // PPW)], 1)
 
         for q in my_send:
-            g.sync.wait_ge(S.cp, NP)
+            g.sync.wait_ge(S["cp%d" % (q // PPW)], PPW)
             g.sync.dma_start(T.land1[slot], T.p_sb[:, cols(q)]).then_inc(S.s1, 16)
-        g.wait_ge(S.cp, NP)
-        trs = []
-        for q in range(NP):
-            d = me["snd"][q]
-            if d == core:
-                continue
-            m = _parts(topo.mask(core, d), NP)[len(trs)]
-            trs.append(RemoteDMATransfer(dst_ids=[_dst(topo, d)], dma_engine_mask=m, remote_sem=S.s1,
-                                         src=T.p_sb[:, cols(q)], dst=T.land1[slot]))
-            loc += _count(m)
-        g.remote_dma_fused(trs, local_sem=S.loc)
+        for v in range(NW):
+            g.wait_ge(S["cp%d" % v], PPW)
+            trs = []
+            for q in range(v * PPW, (v + 1) * PPW):
+                d = me["snd"][q]
+                if d == core:
+                    continue
+                m = _parts(topo.mask(core, d), PPW)[len(trs)]
+                trs.append(RemoteDMATransfer(dst_ids=[_dst(topo, d)], dma_engine_mask=m, remote_sem=S.s1,
+                                             src=T.p_sb[:, cols(q)], dst=T.land1[slot]))
+                loc += _count(m)
+            g.remote_dma_fused(trs, local_sem=S.loc)
 
     for q in my_send:
         need = 0
         for r in me["ranks"]:
-            need += 16 if r == core else _count(_parts(topo.mask(r, core), NP)[0])
+            need += 16 if r == core else _count(_parts(topo.mask(r, core), PPW)[0])
         g.wait_ge(S.s1, need)
         srcs = [T.land1[i] for i in range(len(me["ranks"]))]
         far = [plan[o]["fld"][q] for o in chips if o != ch]

@@ -1,11 +1,14 @@
 from concourse.bass import DstId, RemoteDMATransfer
 
 KT, F = 2, 512
-NP = 4
-PW = F // NP
 NW = 2
-PPW = NP // NW
+NS = 4
+NP = NW * NS
+PW = F // NP
 WW = F // NW
+NB = 4
+BW = F // NB
+BPW = NB // NW
 MAXR = 4
 MAXC = 3
 ADD = 1
@@ -14,17 +17,18 @@ SCRATCH = {
     "a_sb": ("sbuf", [128, KT * 128], "bfloat16"),
     "w_sb": ("sbuf", [128, KT * F], "bfloat16"),
     "p_sb": ("sbuf", [128, F], "bfloat16"),
-    "land1": ("dram", [MAXR, 128, PW], "bfloat16"),
-    "land2": ("dram", [MAXC, 128, PW], "bfloat16"),
+    "land1": ("dram", [NW * MAXR, 128, PW], "bfloat16"),
+    "land2": ("dram", [NW * MAXC, 128, PW], "bfloat16"),
     "fin": ("dram", [NP, 128, PW], "bfloat16"),
 }
-for _q in range(NP):
+for _q in range(NB):
     SCRATCH["ps%d" % _q] = ("psum", [128, 512], "float32")
 
-SEMAPHORES = (["ld_a", "s1", "s2", "loc", "st_a", "st_b"]
+SEMAPHORES = (["ld_a", "loc", "st_a", "st_b"]
               + ["ld_w%d%d" % (_t, _v) for _t in range(KT) for _v in range(NW)]
-              + ["cp%d" % _v for _v in range(NW)]
-              + ["mm%d" % _q for _q in range(NP)] + ["s3_%d" % _q for _q in range(NP)])
+              + ["cp%d" % _v for _v in range(NW)] + ["s1_%d" % _v for _v in range(NW)]
+              + ["s2_%d" % _v for _v in range(NW)]
+              + ["mm%d" % _q for _q in range(NB)] + ["s3_%d" % _q for _q in range(NP)])
 
 
 def _bits(mask):
@@ -52,17 +56,17 @@ def _plan(T, topo):
         ports = [c for c in on[ch] if all(topo.may_write(c, d) for d in away)]
         dies = sorted(set(topo.die(c) for c in ports))
         by_die = [sorted(p for p in ports if topo.die(p) == d) for d in dies]
-        snd = [by_die[d][i] for i in range(NP // len(dies)) for d in range(len(dies))]
+        snd = [by_die[d][i] for i in range(NS // len(dies)) for d in range(len(dies))]
         rk = [c for c in ranks if topo.chip(c) == ch]
         helpers = [c for c in on[ch] if c not in rk]
         idle = [h for h in helpers if h not in snd]
-        fld = [None] * NP
-        hq = [q for q in range(NP) if snd[q] in helpers]
-        for q in range(NP):
-            if q not in hq:
-                fld[q] = idle.pop(0)
-        for i, q in enumerate(hq):
-            fld[q] = snd[hq[(i + 1) % len(hq)]] if len(hq) > 1 else idle.pop(0)
+        fld = [None] * NS
+        hq = [i for i in range(NS) if snd[i] in helpers]
+        for i in range(NS):
+            if i not in hq:
+                fld[i] = idle.pop(0)
+        for j, i in enumerate(hq):
+            fld[i] = snd[hq[(j + 1) % len(hq)]] if len(hq) > 1 else idle.pop(0)
         plan[ch] = {"ranks": rk, "snd": snd, "fld": fld}
     return chips, plan
 
@@ -79,8 +83,8 @@ def rank_program(g, core, T, topo):
         return
     me = plan[ch]
     is_rank = core in me["ranks"]
-    my_send = [q for q in range(NP) if me["snd"][q] == core]
-    my_fold = [q for q in range(NP) if me["fld"][q] == core]
+    my_send = [i for i in range(NS) if me["snd"][i] == core]
+    my_fold = [i for i in range(NS) if me["fld"][i] == core]
     if not (is_rank or my_send or my_fold):
         return
     S = T.sem
@@ -102,73 +106,78 @@ def rank_program(g, core, T, topo):
         for v in range(NW):
             for t in range(KT):
                 te.wait_ge(S["ld_w%d%d" % (t, v)], 16)
-                for q in range(v * PPW, (v + 1) * PPW):
-                    mm = te.matmul(T["ps%d" % q][:, 0:PW], T.a_sb[:, t * 128:(t + 1) * 128],
-                                   T.w_sb[:, t * F + q * PW:t * F + (q + 1) * PW], start=(t == 0), stop=(t == KT - 1))
+                for b in range(v * BPW, (v + 1) * BPW):
+                    mm = te.matmul(T["ps%d" % b][:, 0:BW], T.a_sb[:, t * 128:(t + 1) * 128],
+                                   T.w_sb[:, t * F + b * BW:t * F + (b + 1) * BW], start=(t == 0), stop=(t == KT - 1))
                     if t == KT - 1:
-                        mm.then_inc(S["mm%d" % q], 1)
-        for q in range(NP):
-            g.vector.wait_ge(S["mm%d" % q], 1)
-            g.vector.tensor_copy(T.p_sb[:, cols(q)], T["ps%d" % q][:, 0:PW]).then_inc(S["cp%d" % (q // PPW)], 1)
+                        mm.then_inc(S["mm%d" % b], 1)
+        for b in range(NB):
+            g.vector.wait_ge(S["mm%d" % b], 1)
+            g.vector.tensor_copy(T.p_sb[:, b * BW:(b + 1) * BW], T["ps%d" % b][:, 0:BW]).then_inc(S["cp%d" % (b // BPW)], 1)
 
-        for q in my_send:
-            g.sync.wait_ge(S["cp%d" % (q // PPW)], PPW)
-            g.sync.dma_start(T.land1[slot], T.p_sb[:, cols(q)]).then_inc(S.s1, 16)
         for v in range(NW):
-            g.wait_ge(S["cp%d" % v], PPW)
+            for i in my_send:
+                g.sync.wait_ge(S["cp%d" % v], BPW)
+                g.sync.dma_start(T.land1[v * MAXR + slot], T.p_sb[:, cols(v * NS + i)]).then_inc(S["s1_%d" % v], 16)
+        for v in range(NW):
+            g.wait_ge(S["cp%d" % v], BPW)
             trs = []
-            for q in range(v * PPW, (v + 1) * PPW):
-                d = me["snd"][q]
+            for i in range(NS):
+                d = me["snd"][i]
                 if d == core:
                     continue
-                m = _parts(topo.mask(core, d), PPW)[len(trs)]
-                trs.append(RemoteDMATransfer(dst_ids=[_dst(topo, d)], dma_engine_mask=m, remote_sem=S.s1,
-                                             src=T.p_sb[:, cols(q)], dst=T.land1[slot]))
+                m = _parts(topo.mask(core, d), NS)[len(trs)]
+                trs.append(RemoteDMATransfer(dst_ids=[_dst(topo, d)], dma_engine_mask=m, remote_sem=S["s1_%d" % v],
+                                             src=T.p_sb[:, cols(v * NS + i)], dst=T.land1[v * MAXR + slot]))
                 loc += _count(m)
             g.remote_dma_fused(trs, local_sem=S.loc)
 
-    for q in my_send:
-        need = 0
-        for r in me["ranks"]:
-            need += 16 if r == core else _count(_parts(topo.mask(r, core), PPW)[0])
-        g.wait_ge(S.s1, need)
-        srcs = [T.land1[i] for i in range(len(me["ranks"]))]
-        far = [plan[o]["fld"][q] for o in chips if o != ch]
-        near = me["fld"][q]
-        m_far = topo.mask(core, near)
-        for d in far:
-            m_far &= topo.mask(core, d)
-        m_near = topo.mask(core, near) & ~m_far
-        k = chips.index(ch)
-        trs = [RemoteDMATransfer(dst_ids=[_dst(topo, d) for d in far], dma_engine_mask=m_far, remote_sem=S.s2,
-                                 srcs=srcs, dsts=[T.land2[k] for d in far], alu_op=ADD),
-               RemoteDMATransfer(dst_ids=[_dst(topo, near)], dma_engine_mask=m_near, remote_sem=S.s2,
-                                 srcs=srcs, dsts=[T.land2[k]], alu_op=ADD)]
-        g.remote_dma_fused(trs, local_sem=S.loc)
-        loc += _count(m_far) + _count(m_near)
+    for v in range(NW):
+        for i in my_send:
+            need = 0
+            for r in me["ranks"]:
+                need += 16 if r == core else _count(_parts(topo.mask(r, core), NS)[0])
+            g.wait_ge(S["s1_%d" % v], need)
+            srcs = [T.land1[v * MAXR + k] for k in range(len(me["ranks"]))]
+            far = [plan[o]["fld"][i] for o in chips if o != ch]
+            near = me["fld"][i]
+            m_far = topo.mask(core, near)
+            for d in far:
+                m_far &= topo.mask(core, d)
+            m_near = topo.mask(core, near) & ~m_far
+            k = v * MAXC + chips.index(ch)
+            trs = [RemoteDMATransfer(dst_ids=[_dst(topo, d) for d in far], dma_engine_mask=m_far,
+                                     remote_sem=S["s2_%d" % v], srcs=srcs, dsts=[T.land2[k] for d in far], alu_op=ADD),
+                   RemoteDMATransfer(dst_ids=[_dst(topo, near)], dma_engine_mask=m_near,
+                                     remote_sem=S["s2_%d" % v], srcs=srcs, dsts=[T.land2[k]], alu_op=ADD)]
+            g.remote_dma_fused(trs, local_sem=S.loc)
+            loc += _count(m_far) + _count(m_near)
 
-    for q in my_fold:
-        need = 0
-        for o in chips:
-            s = plan[o]["snd"][q]
-            m_far = topo.mask(s, plan[o]["fld"][q])
-            for o2 in chips:
-                if o2 != o:
-                    m_far &= topo.mask(s, plan[o2]["fld"][q])
-            need += _count(m_far) if o != ch else _count(topo.mask(s, core) & ~m_far)
-        g.wait_ge(S.s2, need)
-        m = topo.mask(core, me["ranks"][0])
-        for r in me["ranks"]:
-            m &= topo.mask(core, r)
-        g.remote_dma_fused([RemoteDMATransfer(dst_ids=[_dst(topo, r) for r in me["ranks"]], dma_engine_mask=m,
-                                              remote_sem=S["s3_%d" % q], srcs=[T.land2[i] for i in range(len(chips))],
-                                              dsts=[T.fin[q] for r in me["ranks"]], alu_op=ADD)], local_sem=S.loc)
-        loc += _count(m)
+    for v in range(NW):
+        for i in my_fold:
+            need = 0
+            for o in chips:
+                s = plan[o]["snd"][i]
+                m_far = topo.mask(s, plan[o]["fld"][i])
+                for o2 in chips:
+                    if o2 != o:
+                        m_far &= topo.mask(s, plan[o2]["fld"][i])
+                need += _count(m_far) if o != ch else _count(topo.mask(s, core) & ~m_far)
+            g.wait_ge(S["s2_%d" % v], need)
+            m = topo.mask(core, me["ranks"][0])
+            for r in me["ranks"]:
+                m &= topo.mask(core, r)
+            q = v * NS + i
+            g.remote_dma_fused([RemoteDMATransfer(dst_ids=[_dst(topo, r) for r in me["ranks"]], dma_engine_mask=m,
+                                                  remote_sem=S["s3_%d" % q],
+                                                  srcs=[T.land2[v * MAXC + k] for k in range(len(chips))],
+                                                  dsts=[T.fin[q] for r in me["ranks"]], alu_op=ADD)], local_sem=S.loc)
+            loc += _count(m)
 
     if is_rank:
         n = [0, 0]
         for q in range(NP):
-            f = me["fld"][q]
+            f = me["fld"][q % NS]
             m = topo.mask(f, core)
             for r in me["ranks"]:
                 m &= topo.mask(f, r)

from concourse.bass import DstId, RemoteDMATransfer

KT, F = 2, 512
NW = 2
NS = 4
NP = NW * NS
PW = F // NP
WW = F // NW
NB = 4
BW = F // NB
BPW = NB // NW
MAXR = 4
MAXC = 3
ADD = 1

SCRATCH = {
    "a_sb": ("sbuf", [128, KT * 128], "bfloat16"),
    "w_sb": ("sbuf", [128, KT * F], "bfloat16"),
    "p_sb": ("sbuf", [128, F], "bfloat16"),
    "land1": ("dram", [NW * MAXR, 128, PW], "bfloat16"),
    "land2": ("dram", [NW * MAXC, 128, PW], "bfloat16"),
    "fin": ("dram", [NP, 128, PW], "bfloat16"),
}
for _q in range(NB):
    SCRATCH["ps%d" % _q] = ("psum", [128, 512], "float32")

SEMAPHORES = (["ld_a", "loc", "st_a", "st_b"]
              + ["ld_w%d%d" % (_t, _v) for _t in range(KT) for _v in range(NW)]
              + ["cp%d" % _v for _v in range(NW)] + ["s1_%d" % _v for _v in range(NW)]
              + ["s2_%d" % _v for _v in range(NW)]
              + ["mm%d" % _q for _q in range(NB)] + ["s3_%d" % _q for _q in range(NP)])


def _bits(mask):
    return [1 << i for i in range(mask.bit_length()) if (mask >> i) & 1]


def _parts(mask, n):
    b = _bits(mask)
    k = len(b) // n
    return [sum(b[i * k:(i + 1) * k]) for i in range(n)]


def _count(mask):
    return len(_bits(mask))


def _plan(T, topo):
    ranks = list(T.cores)
    chips = sorted(set(topo.chip(c) for c in ranks))
    every = range(topo.CHIPS * topo.CORES_PER_CHIP)
    on = dict((ch, [c for c in every if topo.chip(c) == ch]) for ch in chips)
    plan = {}
    for ch in chips:
        away = [d for o in chips if o != ch for d in on[o]]
        ports = [c for c in on[ch] if all(topo.may_write(c, d) for d in away)]
        dies = sorted(set(topo.die(c) for c in ports))
        by_die = [sorted(p for p in ports if topo.die(p) == d) for d in dies]
        snd = [by_die[d][i] for i in range(NS // len(dies)) for d in range(len(dies))]
        rk = [c for c in ranks if topo.chip(c) == ch]
        helpers = [c for c in on[ch] if c not in rk]
        idle = [h for h in helpers if h not in snd]
        fld = [None] * NS
        hq = [i for i in range(NS) if snd[i] in helpers]
        for i in range(NS):
            if i not in hq:
                fld[i] = idle.pop(0)
        for j, i in enumerate(hq):
            fld[i] = snd[hq[(j + 1) % len(hq)]] if len(hq) > 1 else idle.pop(0)
        plan[ch] = {"ranks": rk, "snd": snd, "fld": fld}
    return chips, plan


def _dst(topo, c):
    rid, pid, _se = topo.addr(c)
    return DstId(rid=rid, pnc=pid)


def rank_program(g, core, T, topo):
    chips, plan = _plan(T, topo)
    ch = topo.chip(core)
    if ch not in plan:
        return
    me = plan[ch]
    is_rank = core in me["ranks"]
    my_send = [i for i in range(NS) if me["snd"][i] == core]
    my_fold = [i for i in range(NS) if me["fld"][i] == core]
    if not (is_rank or my_send or my_fold):
        return
    S = T.sem
    loc = 0

    def cols(q):
        return slice(q * PW, (q + 1) * PW)

    if is_rank:
        slot = me["ranks"].index(core)
        g.sync.dma_start(T.a_sb[:], T.a[:]).then_inc(S.ld_a, 16)
        for v in range(NW):
            for t in range(KT):
                qu = (g.scalar, g.sync)[t % 2]
                c0 = t * F + v * WW
                qu.dma_start(T.w_sb[:, c0:c0 + WW], T.w[:, c0:c0 + WW]).then_inc(S["ld_w%d%d" % (t, v)], 16)
        te = g.tensor
        te.wait_ge(S.ld_a, 16)
        for v in range(NW):
            for t in range(KT):
                te.wait_ge(S["ld_w%d%d" % (t, v)], 16)
                for b in range(v * BPW, (v + 1) * BPW):
                    mm = te.matmul(T["ps%d" % b][:, 0:BW], T.a_sb[:, t * 128:(t + 1) * 128],
                                   T.w_sb[:, t * F + b * BW:t * F + (b + 1) * BW], start=(t == 0), stop=(t == KT - 1))
                    if t == KT - 1:
                        mm.then_inc(S["mm%d" % b], 1)
        for b in range(NB):
            g.vector.wait_ge(S["mm%d" % b], 1)
            g.vector.tensor_copy(T.p_sb[:, b * BW:(b + 1) * BW], T["ps%d" % b][:, 0:BW]).then_inc(S["cp%d" % (b // BPW)], 1)

        for v in range(NW):
            for i in my_send:
                g.sync.wait_ge(S["cp%d" % v], BPW)
                g.sync.dma_start(T.land1[v * MAXR + slot], T.p_sb[:, cols(v * NS + i)]).then_inc(S["s1_%d" % v], 16)
        for v in range(NW):
            g.wait_ge(S["cp%d" % v], BPW)
            trs = []
            for i in range(NS):
                d = me["snd"][i]
                if d == core:
                    continue
                m = _parts(topo.mask(core, d), NS)[len(trs)]
                trs.append(RemoteDMATransfer(dst_ids=[_dst(topo, d)], dma_engine_mask=m, remote_sem=S["s1_%d" % v],
                                             src=T.p_sb[:, cols(v * NS + i)], dst=T.land1[v * MAXR + slot]))
                loc += _count(m)
            g.remote_dma_fused(trs, local_sem=S.loc)

    for v in range(NW):
        for i in my_send:
            need = 0
            for r in me["ranks"]:
                need += 16 if r == core else _count(_parts(topo.mask(r, core), NS)[0])
            g.wait_ge(S["s1_%d" % v], need)
            srcs = [T.land1[v * MAXR + k] for k in range(len(me["ranks"]))]
            far = [plan[o]["fld"][i] for o in chips if o != ch]
            near = me["fld"][i]
            m_far = topo.mask(core, near)
            for d in far:
                m_far &= topo.mask(core, d)
            m_near = topo.mask(core, near) & ~m_far
            k = v * MAXC + chips.index(ch)
            trs = [RemoteDMATransfer(dst_ids=[_dst(topo, d) for d in far], dma_engine_mask=m_far,
                                     remote_sem=S["s2_%d" % v], srcs=srcs, dsts=[T.land2[k] for d in far], alu_op=ADD),
                   RemoteDMATransfer(dst_ids=[_dst(topo, near)], dma_engine_mask=m_near,
                                     remote_sem=S["s2_%d" % v], srcs=srcs, dsts=[T.land2[k]], alu_op=ADD)]
            g.remote_dma_fused(trs, local_sem=S.loc)
            loc += _count(m_far) + _count(m_near)

    for v in range(NW):
        for i in my_fold:
            need = 0
            for o in chips:
                s = plan[o]["snd"][i]
                m_far = topo.mask(s, plan[o]["fld"][i])
                for o2 in chips:
                    if o2 != o:
                        m_far &= topo.mask(s, plan[o2]["fld"][i])
                need += _count(m_far) if o != ch else _count(topo.mask(s, core) & ~m_far)
            g.wait_ge(S["s2_%d" % v], need)
            m = topo.mask(core, me["ranks"][0])
            for r in me["ranks"]:
                m &= topo.mask(core, r)
            q = v * NS + i
            g.remote_dma_fused([RemoteDMATransfer(dst_ids=[_dst(topo, r) for r in me["ranks"]], dma_engine_mask=m,
                                                  remote_sem=S["s3_%d" % q],
                                                  srcs=[T.land2[v * MAXC + k] for k in range(len(chips))],
                                                  dsts=[T.fin[q] for r in me["ranks"]], alu_op=ADD)], local_sem=S.loc)
            loc += _count(m)

    if is_rank:
        n = [0, 0]
        for q in range(NP):
            f = me["fld"][q % NS]
            m = topo.mask(f, core)
            for r in me["ranks"]:
                m &= topo.mask(f, r)
            qu, st = ((g.sync, S.st_a), (g.scalar, S.st_b))[q % 2]
            qu.wait_ge(S["s3_%d" % q], _count(m))
            qu.dma_start(T.y[:, cols(q)], T.fin[q]).then_inc(st, 16)
            n[q % 2] += 16
        g.sync.wait_ge(S.st_a, n[0])
        g.scalar.wait_ge(S.st_b, n[1])

    g.wait_ge(S.loc, loc)
